import numpy as np
import ml_dtypes


def mxq(x, axis, fmt="e4m3"):
    dtype, down = {"e4m3": (ml_dtypes.float8_e4m3fn, 7), "e5m2": (ml_dtypes.float8_e5m2, 14)}[fmt]
    v = np.moveaxis(np.asarray(x, np.float32).astype(ml_dtypes.bfloat16).astype(np.float64), axis, -1)
    blocks = v.reshape(v.shape[:-1] + (-1, 32))
    amax = np.abs(blocks).max(-1, keepdims=True)
    byte = np.maximum(np.where(amax > 0, np.frexp(amax)[1] - 1 + 127, 0) - down, 1)
    scale = np.exp2(byte - 127.0)
    codes = (blocks / scale).astype(np.float32).astype(dtype).astype(np.float64)
    return np.moveaxis((codes * scale).reshape(v.shape), -1, axis)


WIDE = False


def mx_kscale(k):
    if not WIDE:
        return np.ones(k)
    levels = np.array([10, -10, 5, -5, 0])
    if k % 512:
        return np.exp2(np.random.permutation(np.resize(levels, k // 32))).repeat(32)
    a = np.empty((k // 512, 16))
    for p in range(k // 512):
        a[p, :8] = np.random.permutation(np.resize(levels, 8))
        for g in range(8):
            far = levels[np.abs(levels - a[p, g]) >= 10]
            a[p, g + 8] = far[np.random.randint(len(far))]
    return np.exp2(a.ravel()).repeat(32)


def f64(x):
    return np.asarray(x).astype(np.float64)


def striped(idx):
    return np.tile(idx.reshape(-1, 16).T, (8, 1)).astype(np.uint16)


def unstriped(offs):
    return offs[:16].T.reshape(-1).astype(np.int64)


def pack_weight(w):
    k, n = w.shape
    w = f64(np.asarray(w, np.float32).astype(ml_dtypes.bfloat16)).reshape(k // 32, 32, n)
    amax = np.abs(w).max(1)
    byte = np.clip(np.where(amax > 0, np.frexp(amax)[1] - 1 + 127 - 7, 1), 1, 254)
    scaled = (w * np.exp2(127.0 - byte)[:, None, :]).reshape(k, n).astype(np.float32)
    words = np.ascontiguousarray(scaled.reshape(k // 512, 128, 4, n).transpose(0, 1, 3, 2)).astype(ml_dtypes.float8_e4m3fn).view(np.uint8)
    return words, np.ascontiguousarray(byte.astype(np.uint8).reshape(k // 512, 16, n))


def unpack_weight(words, scales):
    g, p, n, _ = words.shape
    vals = np.ascontiguousarray(words).view(ml_dtypes.float8_e4m3fn).astype(np.float64) * np.repeat(np.exp2(scales.astype(np.float64) - 127.0), 8, axis=1)[..., None]
    return vals.transpose(0, 1, 3, 2).reshape(g * 512, n)


def relu(v):
    return np.maximum(v, 0.0)


K, T, S, J = 1536, 2048, 512, 256


def setup_inputs():
    n = np.random.standard_normal
    s = mx_kscale(K)[:, None]
    packed_xT = pack_weight(n((K, T)) * s)
    return {
        "x_words": packed_xT[0],
        "x_scales": packed_xT[1],
        "hT": (n((K, J)) / np.sqrt(K) / s).astype(np.float32),
        "gT": (n((K, J)) / np.sqrt(K) / s).astype(np.float32),
        "offs": striped(np.random.permutation(T)[:S]),
    }


def reference(x_words, x_scales, hT, gT, offs):
    hTq = mxq(f64(hT), 0, "e4m3")
    xq = unpack_weight(x_words, x_scales)[:, unstriped(offs)]
    y = hTq.T @ xq
    e = np.exp(y - y.max(axis=1, keepdims=True))
    p = e / e.sum(axis=1, keepdims=True)
    gTq = mxq(f64(gT), 0, "e4m3")
    z = gTq.T @ xq
    e = np.exp(z - z.max(axis=1, keepdims=True))
    q = e / e.sum(axis=1, keepdims=True)
    return relu(p - q)

@@ -1,0 +1,214 @@
+from contextlib import ExitStack
+
+import concourse.mybir as mybir
+
+K, T, S, J = 1536, 2048, 512, 256
+FLOPS = 2 * 2 * K * J * S
+
+F32 = mybir.dt.float32
+BF16 = mybir.dt.bfloat16
+I32 = mybir.dt.int32
+U32 = mybir.dt.uint32
+U16 = mybir.dt.uint16
+U8 = mybir.dt.uint8
+FP8X4 = mybir.dt.float8_e4m3fn_x4
+ACT = mybir.ActivationFunctionType
+ALU = mybir.AluOpType
+AXIS = mybir.AxisListType
+
+P = 128
+PACK = 4
+K_PASS = P * PACK
+PASSES = K // K_PASS
+TILES = J // P
+QUADRANTS = 4
+
+
+def tile_picked_zspec_res_p_kernel(tc, x_words, x_scales, hT, gT, offs, out):
+    nc = tc.nc
+    with ExitStack() as ctx:
+        keep = ctx.enter_context(tc.tile_pool(name="keep", bufs=1))
+        psum = ctx.enter_context(tc.psum_pool(name="psum", bufs=1))
+
+        offsets = keep.tile([P, S // 16], U16, name="offsets")
+        word_table = [keep.tile([P, T], I32, name="word_table%d" % o) for o in range(PASSES)]
+        scale_table = keep.tile([P, T], U8, name="scale_table")
+        warm = keep.tile([P, 8], F32, name="warm")
+
+        nc.vector.memset(scale_table[:].bitcast(I32), 0)
+        nc.vector.memset(warm[:], 0.0)
+        nc.scalar.activation(warm[:, 1:2], warm[:, 0:1], ACT.Exp)
+
+        def load_words(o):
+            nc.sync.dma_start(word_table[o][:], x_words[o].rearrange("p n t -> p (n t)").bitcast(I32))
+
+        load_words(0)
+        nc.sync.dma_start(offsets[:], offs)
+        for q in range(QUADRANTS):
+            nc.gpsimd.dma_start(
+                scale_table[32 * q : 32 * q + 4 * PASSES, :].bitcast(I32),
+                x_scales[:, 4 * q : 4 * q + 4, :].bitcast(I32),
+            )
+        for o in range(1, PASSES):
+            load_words(o)
+
+        raw = {}
+        for m, hidden in enumerate((hT, gT)):
+            for o in range(PASSES):
+                rows = hidden[o * K_PASS : (o + 1) * K_PASS, :].rearrange("(p j) w -> p j w", j=PACK)
+                raw[m, o] = keep.tile([P, PACK, J], F32, name="raw%d_%d" % (m, o))
+                nc.sync.dma_start(raw[m, o][:], rows)
+
+        x_codes = [keep.tile([P, S], U32, name="x_codes%d" % o, align_bytes=64) for o in range(PASSES)]
+        x_planes = keep.tile([P, S], U8, name="x_planes", align_bytes=64)
+        for o in range(PASSES):
+            nc.vector.tensor_copy(x_codes[o][:], word_table[o][:].bitcast(U32).indirect(offsets[:]))
+            if o == 0:
+                nc.vector.tensor_copy(x_planes[:], scale_table[:].indirect(offsets[:]))
+
+        logits, grouped, codes, plane = {}, {}, {}, {}
+        neg_max, sums, inv, expo, prob, diff, result = {}, {}, {}, {}, {}, {}, {}
+        for m in range(2):
+            for o in range(PASSES):
+                codes[m, o] = keep.tile([P, J], U32, name="codes%d_%d" % (m, o), align_bytes=64)
+                plane[m, o] = keep.tile([P, J], U8, name="plane%d_%d" % (m, o), align_bytes=64)
+            for t in range(TILES):
+                logits[m, t] = psum.tile([P, S], F32, name="logits%d_%d" % (m, t))
+                neg_max[m, t] = keep.tile([P, 1], F32, name="neg_max%d_%d" % (m, t))
+                sums[m, t] = keep.tile([P, 1], F32, name="sums%d_%d" % (m, t))
+                inv[m, t] = keep.tile([P, 1], F32, name="inv%d_%d" % (m, t))
+                expo[m, t] = keep.tile([P, S], F32, name="expo%d_%d" % (m, t))
+        for t in range(TILES):
+            diff[t] = keep.tile([P, S], F32, name="diff%d" % t)
+            result[t] = keep.tile([P, S], F32, name="result%d" % t)
+
+        def stage(m, o, t, tag):
+            width = J if t is None else P
+            grouped[m, o, t] = keep.tile([P, width, PACK], BF16, name="grouped%d_%d_%s" % (m, o, t), tag=tag, align_bytes=64)
+
+        def staged(m, o, first, last):
+            if (m, o, None) in grouped:
+                return grouped[m, o, None][:, first:last, :]
+            t = first // P
+            return grouped[m, o, t][:, first - t * P : last - t * P, :]
+
+        def interleave(copy, m, o, first, last):
+            if (m, o) in raw:
+                src = raw[m, o][:, :, first:last]
+            else:
+                t = first // P
+                src = raw[m, o, t][:, :, first - t * P : last - t * P]
+            copy(
+                staged(m, o, first, last).rearrange("p (c i) j -> p c j i", i=4),
+                src.rearrange("p j (c i) -> p c j i", i=4),
+            )
+
+        def quantize(m, o, first, last):
+            nc.vector.quantize_mx(
+                out=codes[m, o][:, first:last].bitcast(FP8X4),
+                scales=plane[m, o][:, first:last],
+                in_=staged(m, o, first, last).rearrange("p c j -> p (c j)"),
+            )
+
+        def multiply(m, o, t):
+            cols = slice(t * P, (t + 1) * P)
+            nc.tensor.matmul_mx(
+                out=logits[m, t][:],
+                lhsT=codes[m, o][:, cols].bitcast(FP8X4),
+                lhsT_scale=plane[m, o][:, cols],
+                rhs=x_codes[o][:].bitcast(FP8X4),
+                rhs_scale=x_planes[4 * o : P, :],
+                start=(o == 0),
+                stop=(o == PASSES - 1),
+            )
+
+        def row_max(m, t):
+            nc.vector.tensor_reduce(neg_max[m, t][:], logits[m, t][:], axis=AXIS.X, op=ALU.max, negate=True)
+
+        def exponentials(m, t):
+            nc.scalar.activation(
+                expo[m, t][:], logits[m, t][:], ACT.Exp, bias=neg_max[m, t][:], scale=1.0, accum_out=sums[m, t][:]
+            )
+
+        def reciprocal(m, t):
+            nc.vector.reciprocal(inv[m, t][:], sums[m, t][:])
+
+        def normalise_v(t):
+            nc.vector.tensor_scalar(prob[t][:], expo[0, t][:], inv[0, t][:], None, op0=ALU.mult)
+
+        def normalise_s(t):
+            nc.scalar.activation(prob[t][:], expo[0, t][:], ACT.Copy, scale=inv[0, t][:])
+
+        def subtract(t, a, b):
+            nc.vector.scalar_tensor_tensor(
+                diff[t][:, a:b], prob[t][:, a:b], sums[1, t][:], expo[1, t][:, a:b], op0=ALU.mult, op1=ALU.subtract
+            )
+
+        def clip_s(t, a, b):
+            nc.scalar.activation(result[t][:, a:b], diff[t][:, a:b], ACT.Relu, scale=inv[1, t][:])
+
+        def clip_v(t, a, b):
+            nc.vector.tensor_scalar(result[t][:, a:b], diff[t][:, a:b], inv[1, t][:], 0.0, op0=ALU.mult, op1=ALU.max)
+
+        def store(engine, t, a, b):
+            engine.dma_start(out[t * P : (t + 1) * P, a:b], result[t][:, a:b])
+
+        on_v, on_s = nc.vector.tensor_copy, nc.scalar.copy
+        for o in range(2):
+            stage(0, o, None, "early%d" % o)
+            interleave(on_v, 0, o, 0, 96)
+            interleave(on_s, 0, o, 96, J)
+            quantize(0, o, 0, J)
+            multiply(0, o, 0)
+            multiply(0, o, 1)
+        stage(0, 2, None, "early2")
+        interleave(on_v, 0, 2, 0, P)
+        interleave(on_s, 0, 2, P, J)
+        for t in range(TILES):
+            quantize(0, 2, t * P, (t + 1) * P)
+            multiply(0, 2, t)
+        stage(1, 0, None, "chain")
+        interleave(on_v, 1, 0, 0, P)
+        interleave(on_s, 1, 0, P, J)
+        row_max(0, 0)
+        exponentials(0, 0)
+        quantize(1, 0, 0, J)
+        multiply(1, 0, 0)
+        multiply(1, 0, 1)
+        stage(1, 1, 0, "chain")
+        stage(1, 1, 1, "side1")
+        interleave(on_v, 1, 1, 0, P)
+        interleave(on_s, 1, 1, P, J)
+        row_max(0, 1)
+        quantize(1, 1, 0, P)
+        multiply(1, 1, 0)
+        stage(1, 2, 0, "chain")
+        stage(1, 2, 1, "side2")
+        interleave(on_v, 1, 2, 0, P)
+        interleave(on_s, 1, 2, P, J)
+        quantize(1, 1, P, J)
+        quantize(1, 2, 0, P)
+        multiply(1, 2, 0)
+        multiply(1, 1, 1)
+        quantize(1, 2, P, J)
+        multiply(1, 2, 1)
+        exponentials(0, 1)
+        reciprocal(0, 0)
+        reciprocal(0, 1)
+        for t in range(TILES):
+            prob[t] = keep.tile([P, S], F32, name="prob%d" % t, tag=("side2", "chain")[t], align_bytes=64)
+            nc.gpsimd.tensor_scalar(prob[t][:], expo[0, t][:], inv[0, t][:], 0.0, op0=ALU.mult, op1=ALU.add)
+        for t in range(TILES):
+            row_max(1, t)
+            exponentials(1, t)
+        reciprocal(1, 0)
+        subtract(0, 0, S)
+        clip_s(0, 0, S)
+        store(nc.sync, 0, 0, S)
+        reciprocal(1, 1)
+        subtract(1, 0, 256)
+        subtract(1, 256, S)
+        clip_s(1, 0, 256)
+        store(nc.scalar, 1, 0, 256)
+        clip_v(1, 256, S)
+        store(nc.sync, 1, 256, S)

@@ -44,13 +44,13 @@ def tile_picked_zspec_res_p_kernel(tc, x_words, x_scales, hT, gT, offs, out):
 
         load_words(0)
         nc.sync.dma_start(offsets[:], offs)
+        load_words(1)
         for q in range(QUADRANTS):
-            nc.gpsimd.dma_start(
+            nc.sync.dma_start(
                 scale_table[32 * q : 32 * q + 4 * PASSES, :].bitcast(I32),
                 x_scales[:, 4 * q : 4 * q + 4, :].bitcast(I32),
             )
-        for o in range(1, PASSES):
-            load_words(o)
+        load_words(2)
 
         raw = {}
         for m, hidden in enumerate((hT, gT)):
@@ -63,7 +63,7 @@ def tile_picked_zspec_res_p_kernel(tc, x_words, x_scales, hT, gT, offs, out):
         x_planes = keep.tile([P, S], U8, name="x_planes", align_bytes=64)
         for o in range(PASSES):
             nc.vector.tensor_copy(x_codes[o][:], word_table[o][:].bitcast(U32).indirect(offsets[:]))
-            if o == 0:
+            if o == 1:
                 nc.vector.tensor_copy(x_planes[:], scale_table[:].indirect(offsets[:]))
 
         logits, grouped, codes, plane = {}, {}, {}, {}

@@ -2,8 +2,8 @@ from contextlib import ExitStack
 
 import concourse.mybir as mybir
 
-K, T, S, J = 1536, 2048, 512, 256
-FLOPS = 2 * 2 * K * J * S
+K, VOCAB, PICKED, POSITIONS = 1536, 2048, 512, 256
+FLOPS = 2 * 2 * K * POSITIONS * PICKED
 
 F32 = mybir.dt.float32
 BF16 = mybir.dt.bfloat16
@@ -20,8 +20,14 @@ P = 128
 PACK = 4
 K_PASS = P * PACK
 PASSES = K // K_PASS
-TILES = J // P
+TILES = POSITIONS // P
+BLOCKS = K_PASS // 32
 QUADRANTS = 4
+ROW_STEP = 2
+LARGE, SMALL = 0, 1
+ALIGN = 64
+EARLY_VECTOR_SHARE = 96
+HALF = PICKED // 2
 
 
 def tile_picked_zspec_res_p_kernel(tc, x_words, x_scales, hT, gT, offs, out):
@@ -30,185 +36,203 @@ def tile_picked_zspec_res_p_kernel(tc, x_words, x_scales, hT, gT, offs, out):
         keep = ctx.enter_context(tc.tile_pool(name="keep", bufs=1))
         psum = ctx.enter_context(tc.psum_pool(name="psum", bufs=1))
 
-        offsets = keep.tile([P, S // 16], U16, name="offsets")
-        word_table = [keep.tile([P, T], I32, name="word_table%d" % o) for o in range(PASSES)]
-        scale_table = keep.tile([P, T], U8, name="scale_table")
-        warm = keep.tile([P, 8], F32, name="warm")
+        def sbuf(shape, dtype, name, tag=None):
+            return keep.tile(shape, dtype, name=name, tag=tag or name, align_bytes=ALIGN)
+
+        offsets = keep.tile([P, PICKED // 16], U16, name="offsets")
+        word_table = [sbuf([P, VOCAB], I32, "word_table%d" % o) for o in range(PASSES)]
+        scale_table = sbuf([P, VOCAB], U8, "scale_table")
+        x_planes = sbuf([P, PASSES * PICKED], U8, "x_planes")
 
         nc.vector.memset(scale_table[:].bitcast(I32), 0)
-        nc.vector.memset(warm[:], 0.0)
-        nc.scalar.activation(warm[:, 1:2], warm[:, 0:1], ACT.Exp)
+        nc.vector.memset(x_planes[:].bitcast(I32), 0)
 
-        def load_words(o):
-            nc.sync.dma_start(word_table[o][:], x_words[o].rearrange("p n t -> p (n t)").bitcast(I32))
+        rows = {}
 
-        load_words(0)
+        def load_rows(model, o, tag=None):
+            hidden = (hT, gT)[model][o * K_PASS : (o + 1) * K_PASS, :]
+            rows[model, o] = sbuf([P, PACK, POSITIONS], F32, "rows%d_%d" % (model, o), tag)
+            nc.sync.dma_start(rows[model, o][:], hidden.rearrange("(p j) w -> p j w", j=PACK))
+
+        load_rows(LARGE, 0)
         nc.sync.dma_start(offsets[:], offs)
-        load_words(1)
+        load_rows(LARGE, 1)
+        nc.sync.dma_start(
+            scale_table[0 : ROW_STEP * BLOCKS * PASSES : ROW_STEP, :].bitcast(I32),
+            x_scales.rearrange("o b c -> b o c").bitcast(I32),
+        )
+        for o in range(PASSES):
+            nc.sync.dma_start(word_table[o][:], x_words[o].rearrange("p n j -> p (n j)").bitcast(I32))
+
+        picked_scales = sbuf([P, PICKED], U8, "picked_scales")
+        nc.vector.tensor_copy(picked_scales[:], scale_table[:].indirect(offsets[:]))
+        span = ROW_STEP * PASSES * BLOCKS // QUADRANTS
         for q in range(QUADRANTS):
             nc.sync.dma_start(
-                scale_table[32 * q : 32 * q + 4 * PASSES, :].bitcast(I32),
-                x_scales[:, 4 * q : 4 * q + 4, :].bitcast(I32),
+                x_planes[32 * q : 32 * q + 4, :].bitcast(I32),
+                picked_scales[span * q : span * (q + 1) : ROW_STEP, :].bitcast(I32),
             )
-        load_words(2)
 
-        raw = {}
-        for m, hidden in enumerate((hT, gT)):
-            for o in range(PASSES):
-                rows = hidden[o * K_PASS : (o + 1) * K_PASS, :].rearrange("(p j) w -> p j w", j=PACK)
-                raw[m, o] = keep.tile([P, PACK, J], F32, name="raw%d_%d" % (m, o))
-                nc.sync.dma_start(raw[m, o][:], rows)
-
-        x_codes = [keep.tile([P, S], U32, name="x_codes%d" % o, align_bytes=64) for o in range(PASSES)]
-        x_planes = keep.tile([P, S], U8, name="x_planes", align_bytes=64)
+        load_rows(LARGE, 2, "scale_table")
+        x_codes = [sbuf([P, PICKED], U32, "x_codes%d" % o) for o in range(PASSES)]
         for o in range(PASSES):
             nc.vector.tensor_copy(x_codes[o][:], word_table[o][:].bitcast(U32).indirect(offsets[:]))
-            if o == 1:
-                nc.vector.tensor_copy(x_planes[:], scale_table[:].indirect(offsets[:]))
+            load_rows(SMALL, o, "word_table%d" % o)
 
-        logits, grouped, codes, plane = {}, {}, {}, {}
-        neg_max, sums, inv, expo, prob, diff, result = {}, {}, {}, {}, {}, {}, {}
-        for m in range(2):
+        logits, codes, plane = {}, {}, {}
+        neg_max, sums, inv_sums, exps = {}, {}, {}, {}
+        for model in (LARGE, SMALL):
             for o in range(PASSES):
-                codes[m, o] = keep.tile([P, J], U32, name="codes%d_%d" % (m, o), align_bytes=64)
-                plane[m, o] = keep.tile([P, J], U8, name="plane%d_%d" % (m, o), align_bytes=64)
+                codes[model, o] = sbuf([P, POSITIONS], U32, "codes%d_%d" % (model, o))
+                plane[model, o] = sbuf([P, POSITIONS], U8, "plane%d_%d" % (model, o))
             for t in range(TILES):
-                logits[m, t] = psum.tile([P, S], F32, name="logits%d_%d" % (m, t))
-                neg_max[m, t] = keep.tile([P, 1], F32, name="neg_max%d_%d" % (m, t))
-                sums[m, t] = keep.tile([P, 1], F32, name="sums%d_%d" % (m, t))
-                inv[m, t] = keep.tile([P, 1], F32, name="inv%d_%d" % (m, t))
-                expo[m, t] = keep.tile([P, S], F32, name="expo%d_%d" % (m, t))
-        for t in range(TILES):
-            diff[t] = keep.tile([P, S], F32, name="diff%d" % t)
-            result[t] = keep.tile([P, S], F32, name="result%d" % t)
+                logits[model, t] = psum.tile([P, PICKED], F32, name="logits%d_%d" % (model, t))
+                neg_max[model, t] = sbuf([P, 1], F32, "neg_max%d_%d" % (model, t))
+                sums[model, t] = sbuf([P, 1], F32, "sums%d_%d" % (model, t))
+                inv_sums[model, t] = sbuf([P, 1], F32, "inv_sums%d_%d" % (model, t))
+                exps[model, t] = sbuf([P, PICKED], F32, "exps%d_%d" % (model, t))
+        diff = [sbuf([P, PICKED], F32, "diff%d" % t) for t in range(TILES)]
+        result = [sbuf([P, PICKED], F32, "result%d" % t) for t in range(TILES)]
 
-        def stage(m, o, t, tag):
-            width = J if t is None else P
-            grouped[m, o, t] = keep.tile([P, width, PACK], BF16, name="grouped%d_%d_%s" % (m, o, t), tag=tag, align_bytes=64)
+        staged = {}
 
-        def staged(m, o, first, last):
-            if (m, o, None) in grouped:
-                return grouped[m, o, None][:, first:last, :]
-            t = first // P
-            return grouped[m, o, t][:, first - t * P : last - t * P, :]
+        def stage_pass(model, o, tag=None):
+            both = sbuf([P, POSITIONS, PACK], BF16, "staged%d_%d" % (model, o), tag)
+            for t in range(TILES):
+                staged[model, o, t] = both[:, t * P : (t + 1) * P, :]
+            return both
 
-        def interleave(copy, m, o, first, last):
-            if (m, o) in raw:
-                src = raw[m, o][:, :, first:last]
-            else:
-                t = first // P
-                src = raw[m, o, t][:, :, first - t * P : last - t * P]
-            copy(
-                staged(m, o, first, last).rearrange("p (c i) j -> p c j i", i=4),
-                src.rearrange("p j (c i) -> p c j i", i=4),
-            )
+        def stage_tile(model, o, t, tag=None):
+            staged[model, o, t] = sbuf([P, P, PACK], BF16, "staged%d_%d_%d" % (model, o, t), tag)[:]
 
-        def quantize(m, o, first, last):
+        def copy_by_activation(dst, src):
+            nc.scalar.activation(dst, src, ACT.Copy)
+
+        def interleave(copy, dst, src):
+            copy(dst.rearrange("p (c i) j -> p c j i", i=4), src.rearrange("p j (c i) -> p c j i", i=4))
+
+        def interleave_tiles(model, o):
+            for t, copy in enumerate((nc.vector.tensor_copy, nc.scalar.copy)):
+                interleave(copy, staged[model, o, t], rows[model, o][:, :, t * P : (t + 1) * P])
+
+        def quantize(model, o, cols, values):
             nc.vector.quantize_mx(
-                out=codes[m, o][:, first:last].bitcast(FP8X4),
-                scales=plane[m, o][:, first:last],
-                in_=staged(m, o, first, last).rearrange("p c j -> p (c j)"),
+                out=codes[model, o][:, cols].bitcast(FP8X4),
+                scales=plane[model, o][:, cols],
+                in_=values.rearrange("p c j -> p (c j)"),
             )
 
-        def multiply(m, o, t):
+        def quantize_tile(model, o, t):
+            quantize(model, o, slice(t * P, (t + 1) * P), staged[model, o, t])
+
+        def multiply(model, o, t, last_pass=PASSES - 1):
             cols = slice(t * P, (t + 1) * P)
             nc.tensor.matmul_mx(
-                out=logits[m, t][:],
-                lhsT=codes[m, o][:, cols].bitcast(FP8X4),
-                lhsT_scale=plane[m, o][:, cols],
+                out=logits[model, t][:],
+                lhsT=codes[model, o][:, cols].bitcast(FP8X4),
+                lhsT_scale=plane[model, o][:, cols],
                 rhs=x_codes[o][:].bitcast(FP8X4),
-                rhs_scale=x_planes[4 * o : P, :],
+                rhs_scale=x_planes[:, o * PICKED : (o + 1) * PICKED],
                 start=(o == 0),
-                stop=(o == PASSES - 1),
+                stop=(o == last_pass),
             )
 
-        def row_max(m, t):
-            nc.vector.tensor_reduce(neg_max[m, t][:], logits[m, t][:], axis=AXIS.X, op=ALU.max, negate=True)
+        def row_max(model, t):
+            nc.vector.tensor_reduce(neg_max[model, t][:], logits[model, t][:], axis=AXIS.X, op=ALU.max, negate=True)
 
-        def exponentials(m, t):
+        def exponentials(model, t):
             nc.scalar.activation(
-                expo[m, t][:], logits[m, t][:], ACT.Exp, bias=neg_max[m, t][:], scale=1.0, accum_out=sums[m, t][:]
+                exps[model, t][:],
+                logits[model, t][:],
+                ACT.Exp,
+                bias=neg_max[model, t][:],
+                scale=1.0,
+                accum_out=sums[model, t][:],
             )
 
-        def reciprocal(m, t):
-            nc.vector.reciprocal(inv[m, t][:], sums[m, t][:])
+        def reciprocal(model, t):
+            nc.vector.reciprocal(inv_sums[model, t][:], sums[model, t][:])
 
-        def normalise_v(t):
-            nc.vector.tensor_scalar(prob[t][:], expo[0, t][:], inv[0, t][:], None, op0=ALU.mult)
+        for o, scalar_copy in enumerate((copy_by_activation, nc.scalar.copy)):
+            both = stage_pass(LARGE, o)
+            split = EARLY_VECTOR_SHARE
+            interleave(nc.vector.tensor_copy, both[:, :split, :], rows[LARGE, o][:, :, :split])
+            interleave(scalar_copy, both[:, split:, :], rows[LARGE, o][:, :, split:])
+            quantize(LARGE, o, slice(0, POSITIONS), both[:])
+            multiply(LARGE, o, 0)
+        multiply(LARGE, 0, 1, last_pass=1)
+        stage_pass(LARGE, 2)
+        interleave_tiles(LARGE, 2)
+        quantize_tile(LARGE, 2, 0)
+        multiply(LARGE, 2, 0)
+        quantize_tile(LARGE, 2, 1)
+        multiply(LARGE, 2, 1, last_pass=1)
+        multiply(LARGE, 1, 1, last_pass=1)
 
-        def normalise_s(t):
-            nc.scalar.activation(prob[t][:], expo[0, t][:], ACT.Copy, scale=inv[0, t][:])
+        both = stage_pass(SMALL, 0, "chain")
+        interleave_tiles(SMALL, 0)
+        row_max(LARGE, 0)
+        exponentials(LARGE, 0)
+        quantize(SMALL, 0, slice(0, POSITIONS), both[:])
+        for t in range(TILES):
+            multiply(SMALL, 0, t)
+        stage_tile(SMALL, 1, 0, "chain")
+        stage_tile(SMALL, 1, 1)
+        interleave_tiles(SMALL, 1)
+        row_max(LARGE, 1)
+        quantize_tile(SMALL, 1, 0)
+        multiply(SMALL, 1, 0)
+        stage_tile(SMALL, 2, 0, "chain")
+        stage_tile(SMALL, 2, 1, "last_staged")
+        interleave_tiles(SMALL, 2)
+        quantize_tile(SMALL, 1, 1)
+        quantize_tile(SMALL, 2, 0)
+        multiply(SMALL, 2, 0)
+        multiply(SMALL, 1, 1)
+        quantize_tile(SMALL, 2, 1)
+        multiply(SMALL, 2, 1)
+        exponentials(LARGE, 1)
 
-        def subtract(t, a, b):
+        for t in range(TILES):
+            reciprocal(LARGE, t)
+        prob = []
+        for t, tag in enumerate(("last_staged", "chain")):
+            prob.append(sbuf([P, PICKED], F32, "prob%d" % t, tag))
+            nc.gpsimd.tensor_scalar(prob[t][:], exps[LARGE, t][:], inv_sums[LARGE, t][:], 0.0, op0=ALU.mult, op1=ALU.add)
+        for t in range(TILES):
+            row_max(SMALL, t)
+            exponentials(SMALL, t)
+
+        def subtract(t, cols):
             nc.vector.scalar_tensor_tensor(
-                diff[t][:, a:b], prob[t][:, a:b], sums[1, t][:], expo[1, t][:, a:b], op0=ALU.mult, op1=ALU.subtract
+                diff[t][:, cols],
+                prob[t][:, cols],
+                sums[SMALL, t][:],
+                exps[SMALL, t][:, cols],
+                op0=ALU.mult,
+                op1=ALU.subtract,
             )
 
-        def clip_s(t, a, b):
-            nc.scalar.activation(result[t][:, a:b], diff[t][:, a:b], ACT.Relu, scale=inv[1, t][:])
+        def clip_on_scalar(t, cols):
+            nc.scalar.activation(result[t][:, cols], diff[t][:, cols], ACT.Relu, scale=inv_sums[SMALL, t][:])
 
-        def clip_v(t, a, b):
-            nc.vector.tensor_scalar(result[t][:, a:b], diff[t][:, a:b], inv[1, t][:], 0.0, op0=ALU.mult, op1=ALU.max)
+        def clip_on_vector(t, cols):
+            nc.vector.tensor_scalar(
+                result[t][:, cols], diff[t][:, cols], inv_sums[SMALL, t][:], 0.0, op0=ALU.mult, op1=ALU.max
+            )
 
-        def store(engine, t, a, b):
-            engine.dma_start(out[t * P : (t + 1) * P, a:b], result[t][:, a:b])
+        def store(engine, t, cols):
+            engine.dma_start(out[t * P : (t + 1) * P, cols], result[t][:, cols])
 
-        on_v, on_s = nc.vector.tensor_copy, nc.scalar.copy
-        for o in range(2):
-            stage(0, o, None, "early%d" % o)
-            interleave(on_v, 0, o, 0, 96)
-            interleave(on_s, 0, o, 96, J)
-            quantize(0, o, 0, J)
-            multiply(0, o, 0)
-            multiply(0, o, 1)
-        stage(0, 2, None, "early2")
-        interleave(on_v, 0, 2, 0, P)
-        interleave(on_s, 0, 2, P, J)
-        for t in range(TILES):
-            quantize(0, 2, t * P, (t + 1) * P)
-            multiply(0, 2, t)
-        stage(1, 0, None, "chain")
-        interleave(on_v, 1, 0, 0, P)
-        interleave(on_s, 1, 0, P, J)
-        row_max(0, 0)
-        exponentials(0, 0)
-        quantize(1, 0, 0, J)
-        multiply(1, 0, 0)
-        multiply(1, 0, 1)
-        stage(1, 1, 0, "chain")
-        stage(1, 1, 1, "side1")
-        interleave(on_v, 1, 1, 0, P)
-        interleave(on_s, 1, 1, P, J)
-        row_max(0, 1)
-        quantize(1, 1, 0, P)
-        multiply(1, 1, 0)
-        stage(1, 2, 0, "chain")
-        stage(1, 2, 1, "side2")
-        interleave(on_v, 1, 2, 0, P)
-        interleave(on_s, 1, 2, P, J)
-        quantize(1, 1, P, J)
-        quantize(1, 2, 0, P)
-        multiply(1, 2, 0)
-        multiply(1, 1, 1)
-        quantize(1, 2, P, J)
-        multiply(1, 2, 1)
-        exponentials(0, 1)
-        reciprocal(0, 0)
-        reciprocal(0, 1)
-        for t in range(TILES):
-            prob[t] = keep.tile([P, S], F32, name="prob%d" % t, tag=("side2", "chain")[t], align_bytes=64)
-            nc.gpsimd.tensor_scalar(prob[t][:], expo[0, t][:], inv[0, t][:], 0.0, op0=ALU.mult, op1=ALU.add)
-        for t in range(TILES):
-            row_max(1, t)
-            exponentials(1, t)
-        reciprocal(1, 0)
-        subtract(0, 0, S)
-        clip_s(0, 0, S)
-        store(nc.sync, 0, 0, S)
-        reciprocal(1, 1)
-        subtract(1, 0, 256)
-        subtract(1, 256, S)
-        clip_s(1, 0, 256)
-        store(nc.scalar, 1, 0, 256)
-        clip_v(1, 256, S)
-        store(nc.sync, 1, 256, S)
+        whole, left, right = slice(0, PICKED), slice(0, HALF), slice(HALF, PICKED)
+        reciprocal(SMALL, 0)
+        subtract(0, whole)
+        clip_on_scalar(0, whole)
+        store(nc.sync, 0, whole)
+        reciprocal(SMALL, 1)
+        subtract(1, left)
+        subtract(1, right)
+        clip_on_scalar(1, left)
+        store(nc.scalar, 1, left)
+        clip_on_vector(1, right)
+        store(nc.sync, 1, right)

from contextlib import ExitStack

import concourse.mybir as mybir

K, VOCAB, PICKED, POSITIONS = 1536, 2048, 512, 256
FLOPS = 2 * 2 * K * POSITIONS * PICKED

F32 = mybir.dt.float32
BF16 = mybir.dt.bfloat16
I32 = mybir.dt.int32
U32 = mybir.dt.uint32
U16 = mybir.dt.uint16
U8 = mybir.dt.uint8
FP8X4 = mybir.dt.float8_e4m3fn_x4
ACT = mybir.ActivationFunctionType
ALU = mybir.AluOpType
AXIS = mybir.AxisListType

P = 128
PACK = 4
K_PASS = P * PACK
PASSES = K // K_PASS
TILES = POSITIONS // P
BLOCKS = K_PASS // 32
QUADRANTS = 4
ROW_STEP = 2
LARGE, SMALL = 0, 1
ALIGN = 64
EARLY_VECTOR_SHARE = 96
HALF = PICKED // 2


def tile_picked_zspec_res_p_kernel(tc, x_words, x_scales, hT, gT, offs, out):
    nc = tc.nc
    with ExitStack() as ctx:
        keep = ctx.enter_context(tc.tile_pool(name="keep", bufs=1))
        psum = ctx.enter_context(tc.psum_pool(name="psum", bufs=1))

        def sbuf(shape, dtype, name, tag=None):
            return keep.tile(shape, dtype, name=name, tag=tag or name, align_bytes=ALIGN)

        offsets = keep.tile([P, PICKED // 16], U16, name="offsets")
        word_table = [sbuf([P, VOCAB], I32, "word_table%d" % o) for o in range(PASSES)]
        scale_table = sbuf([P, VOCAB], U8, "scale_table")
        x_planes = sbuf([P, PASSES * PICKED], U8, "x_planes")

        nc.vector.memset(scale_table[:].bitcast(I32), 0)
        nc.vector.memset(x_planes[:].bitcast(I32), 0)

        rows = {}

        def load_rows(model, o, tag=None):
            hidden = (hT, gT)[model][o * K_PASS : (o + 1) * K_PASS, :]
            rows[model, o] = sbuf([P, PACK, POSITIONS], F32, "rows%d_%d" % (model, o), tag)
            nc.sync.dma_start(rows[model, o][:], hidden.rearrange("(p j) w -> p j w", j=PACK))

        load_rows(LARGE, 0)
        nc.sync.dma_start(offsets[:], offs)
        load_rows(LARGE, 1)
        nc.sync.dma_start(
            scale_table[0 : ROW_STEP * BLOCKS * PASSES : ROW_STEP, :].bitcast(I32),
            x_scales.rearrange("o b c -> b o c").bitcast(I32),
        )
        for o in range(PASSES):
            nc.sync.dma_start(word_table[o][:], x_words[o].rearrange("p n j -> p (n j)").bitcast(I32))

        picked_scales = sbuf([P, PICKED], U8, "picked_scales")
        nc.vector.tensor_copy(picked_scales[:], scale_table[:].indirect(offsets[:]))
        span = ROW_STEP * PASSES * BLOCKS // QUADRANTS
        for q in range(QUADRANTS):
            nc.sync.dma_start(
                x_planes[32 * q : 32 * q + 4, :].bitcast(I32),
                picked_scales[span * q : span * (q + 1) : ROW_STEP, :].bitcast(I32),
            )

        load_rows(LARGE, 2, "scale_table")
        x_codes = [sbuf([P, PICKED], U32, "x_codes%d" % o) for o in range(PASSES)]
        for o in range(PASSES):
            nc.vector.tensor_copy(x_codes[o][:], word_table[o][:].bitcast(U32).indirect(offsets[:]))
            load_rows(SMALL, o, "word_table%d" % o)

        logits, codes, plane = {}, {}, {}
        neg_max, sums, inv_sums, exps = {}, {}, {}, {}
        for model in (LARGE, SMALL):
            for o in range(PASSES):
                codes[model, o] = sbuf([P, POSITIONS], U32, "codes%d_%d" % (model, o))
                plane[model, o] = sbuf([P, POSITIONS], U8, "plane%d_%d" % (model, o))
            for t in range(TILES):
                logits[model, t] = psum.tile([P, PICKED], F32, name="logits%d_%d" % (model, t))
                neg_max[model, t] = sbuf([P, 1], F32, "neg_max%d_%d" % (model, t))
                sums[model, t] = sbuf([P, 1], F32, "sums%d_%d" % (model, t))
                inv_sums[model, t] = sbuf([P, 1], F32, "inv_sums%d_%d" % (model, t))
                exps[model, t] = sbuf([P, PICKED], F32, "exps%d_%d" % (model, t))
        diff = [sbuf([P, PICKED], F32, "diff%d" % t) for t in range(TILES)]
        result = [sbuf([P, PICKED], F32, "result%d" % t) for t in range(TILES)]

        staged = {}

        def stage_pass(model, o, tag=None):
            both = sbuf([P, POSITIONS, PACK], BF16, "staged%d_%d" % (model, o), tag)
            for t in range(TILES):
                staged[model, o, t] = both[:, t * P : (t + 1) * P, :]
            return both

        def stage_tile(model, o, t, tag=None):
            staged[model, o, t] = sbuf([P, P, PACK], BF16, "staged%d_%d_%d" % (model, o, t), tag)[:]

        def copy_by_activation(dst, src):
            nc.scalar.activation(dst, src, ACT.Copy)

        def interleave(copy, dst, src):
            copy(dst.rearrange("p (c i) j -> p c j i", i=4), src.rearrange("p j (c i) -> p c j i", i=4))

        def interleave_tiles(model, o):
            for t, copy in enumerate((nc.vector.tensor_copy, nc.scalar.copy)):
                interleave(copy, staged[model, o, t], rows[model, o][:, :, t * P : (t + 1) * P])

        def quantize(model, o, cols, values):
            nc.vector.quantize_mx(
                out=codes[model, o][:, cols].bitcast(FP8X4),
                scales=plane[model, o][:, cols],
                in_=values.rearrange("p c j -> p (c j)"),
            )

        def quantize_tile(model, o, t):
            quantize(model, o, slice(t * P, (t + 1) * P), staged[model, o, t])

        def multiply(model, o, t, last_pass=PASSES - 1):
            cols = slice(t * P, (t + 1) * P)
            nc.tensor.matmul_mx(
                out=logits[model, t][:],
                lhsT=codes[model, o][:, cols].bitcast(FP8X4),
                lhsT_scale=plane[model, o][:, cols],
                rhs=x_codes[o][:].bitcast(FP8X4),
                rhs_scale=x_planes[:, o * PICKED : (o + 1) * PICKED],
                start=(o == 0),
                stop=(o == last_pass),
            )

        def row_max(model, t):
            nc.vector.tensor_reduce(neg_max[model, t][:], logits[model, t][:], axis=AXIS.X, op=ALU.max, negate=True)

        def exponentials(model, t):
            nc.scalar.activation(
                exps[model, t][:],
                logits[model, t][:],
                ACT.Exp,
                bias=neg_max[model, t][:],
                scale=1.0,
                accum_out=sums[model, t][:],
            )

        def reciprocal(model, t):
            nc.vector.reciprocal(inv_sums[model, t][:], sums[model, t][:])

        for o, scalar_copy in enumerate((copy_by_activation, nc.scalar.copy)):
            both = stage_pass(LARGE, o)
            split = EARLY_VECTOR_SHARE
            interleave(nc.vector.tensor_copy, both[:, :split, :], rows[LARGE, o][:, :, :split])
            interleave(scalar_copy, both[:, split:, :], rows[LARGE, o][:, :, split:])
            quantize(LARGE, o, slice(0, POSITIONS), both[:])
            multiply(LARGE, o, 0)
        multiply(LARGE, 0, 1, last_pass=1)
        stage_pass(LARGE, 2)
        interleave_tiles(LARGE, 2)
        quantize_tile(LARGE, 2, 0)
        multiply(LARGE, 2, 0)
        quantize_tile(LARGE, 2, 1)
        multiply(LARGE, 2, 1, last_pass=1)
        multiply(LARGE, 1, 1, last_pass=1)

        both = stage_pass(SMALL, 0, "chain")
        interleave_tiles(SMALL, 0)
        row_max(LARGE, 0)
        exponentials(LARGE, 0)
        quantize(SMALL, 0, slice(0, POSITIONS), both[:])
        for t in range(TILES):
            multiply(SMALL, 0, t)
        stage_tile(SMALL, 1, 0, "chain")
        stage_tile(SMALL, 1, 1)
        interleave_tiles(SMALL, 1)
        row_max(LARGE, 1)
        quantize_tile(SMALL, 1, 0)
        multiply(SMALL, 1, 0)
        stage_tile(SMALL, 2, 0, "chain")
        stage_tile(SMALL, 2, 1, "last_staged")
        interleave_tiles(SMALL, 2)
        quantize_tile(SMALL, 1, 1)
        quantize_tile(SMALL, 2, 0)
        multiply(SMALL, 2, 0)
        multiply(SMALL, 1, 1)
        quantize_tile(SMALL, 2, 1)
        multiply(SMALL, 2, 1)
        exponentials(LARGE, 1)

        for t in range(TILES):
            reciprocal(LARGE, t)
        prob = []
        for t, tag in enumerate(("last_staged", "chain")):
            prob.append(sbuf([P, PICKED], F32, "prob%d" % t, tag))
            nc.gpsimd.tensor_scalar(prob[t][:], exps[LARGE, t][:], inv_sums[LARGE, t][:], 0.0, op0=ALU.mult, op1=ALU.add)
        for t in range(TILES):
            row_max(SMALL, t)
            exponentials(SMALL, t)

        def subtract(t, cols):
            nc.vector.scalar_tensor_tensor(
                diff[t][:, cols],
                prob[t][:, cols],
                sums[SMALL, t][:],
                exps[SMALL, t][:, cols],
                op0=ALU.mult,
                op1=ALU.subtract,
            )

        def clip_on_scalar(t, cols):
            nc.scalar.activation(result[t][:, cols], diff[t][:, cols], ACT.Relu, scale=inv_sums[SMALL, t][:])

        def clip_on_vector(t, cols):
            nc.vector.tensor_scalar(
                result[t][:, cols], diff[t][:, cols], inv_sums[SMALL, t][:], 0.0, op0=ALU.mult, op1=ALU.max
            )

        def store(engine, t, cols):
            engine.dma_start(out[t * P : (t + 1) * P, cols], result[t][:, cols])

        whole, left, right = slice(0, PICKED), slice(0, HALF), slice(HALF, PICKED)
        reciprocal(SMALL, 0)
        subtract(0, whole)
        clip_on_scalar(0, whole)
        store(nc.sync, 0, whole)
        reciprocal(SMALL, 1)
        subtract(1, left)
        subtract(1, right)
        clip_on_scalar(1, left)
        store(nc.scalar, 1, left)
        clip_on_vector(1, right)
        store(nc.sync, 1, right)
